import numpy as np
import ml_dtypes


def mxq(x, axis, fmt="e4m3"):
    dtype, down = {"e4m3": (ml_dtypes.float8_e4m3fn, 7), "e5m2": (ml_dtypes.float8_e5m2, 14)}[fmt]
    v = np.moveaxis(np.asarray(x, np.float32).astype(ml_dtypes.bfloat16).astype(np.float64), axis, -1)
    blocks = v.reshape(v.shape[:-1] + (-1, 32))
    amax = np.abs(blocks).max(-1, keepdims=True)
    byte = np.maximum(np.where(amax > 0, np.frexp(amax)[1] - 1 + 127, 0) - down, 1)
    scale = np.exp2(byte - 127.0)
    codes = (blocks / scale).astype(np.float32).astype(dtype).astype(np.float64)
    return np.moveaxis((codes * scale).reshape(v.shape), -1, axis)


WIDE = False


def mx_kscale(k):
    if not WIDE:
        return np.ones(k)
    levels = np.array([10, -10, 5, -5, 0])
    if k % 512:
        return np.exp2(np.random.permutation(np.resize(levels, k // 32))).repeat(32)
    a = np.empty((k // 512, 16))
    for p in range(k // 512):
        a[p, :8] = np.random.permutation(np.resize(levels, 8))
        for g in range(8):
            far = levels[np.abs(levels - a[p, g]) >= 10]
            a[p, g + 8] = far[np.random.randint(len(far))]
    return np.exp2(a.ravel()).repeat(32)


BF16 = ml_dtypes.bfloat16


def bf(x):
    return np.asarray(x, np.float32).astype(BF16)


def f64(x):
    return np.asarray(x).astype(np.float64)

E4M3FN = np.array([(-1.0 if i & 128 else 1.0) * ((1.0 + (i & 7) / 8.0) * 2.0 ** (((i >> 3) & 15) - 7) if i & 120 else (i & 7) * 2.0 ** -9) for i in range(256)])


def e4m3fn_bytes(y):
    return np.clip(np.asarray(y, np.float64), -448.0, 448.0).astype(np.float32).astype(ml_dtypes.float8_e4m3fn).view(np.uint8)


def e4m3fn_values(b):
    return E4M3FN[b]

def planes(Y):
    n, m = Y.shape
    b = f64(bf(Y)).reshape(n // 32, 32, m)
    amax = np.abs(b).max(1)
    byte = np.clip(np.where(amax > 0, np.frexp(amax)[1] - 1 + 127 - 7, 1), 1, 254)
    codes = (b * np.exp2(127.0 - byte)[:, None, :]).reshape(n, m).astype(np.float32).astype(ml_dtypes.float8_e4m3fn).view(np.uint8)
    words = codes.reshape(n // 512, 128, 4, m).transpose(0, 1, 3, 2)
    return np.ascontiguousarray(words), np.ascontiguousarray(byte.astype(np.uint8).reshape(n // 512, 16, m))


T, F, H, B = 1024, 2048, 1024, 128


def setup_inputs():
    s = mx_kscale(F)
    t = mx_kscale(H)
    X = 0.8 * np.random.randn(T, F) / s
    W = 1.5 * np.random.randn(F, H) / np.sqrt(F) * s[:, None] * t[None, :]
    W_scale = (np.abs(W).reshape(F, H // B, B).max(axis=2) / 448.0).astype(np.float32)
    W_bytes = e4m3fn_bytes(W / np.repeat(f64(W_scale), B, axis=1))
    enc_gain = np.exp(0.3 * np.random.randn(1, H)) / t
    code_gain = np.exp(0.3 * np.random.randn(1, H)) / t
    dec_gain = np.exp(0.3 * np.random.randn(1, F)) / (s * s)
    V = np.exp(0.7 * np.random.randn(T, 1) + 0.4 * np.random.randn(1, F) + 0.3 * np.random.randn(T, F)) * s
    return {"X": bf(X), "W_bytes": W_bytes, "W_scale": W_scale,
            "enc_gain": bf(enc_gain), "code_gain": bf(code_gain),
            "dec_gain": bf(dec_gain), "V": bf(V)}

def reference(X, W_bytes, W_scale, enc_gain, code_gain, dec_gain, V):
    X = f64(X)
    W = e4m3fn_values(W_bytes) * np.repeat(f64(W_scale), B, axis=1)
    Z = mxq(X, 1) @ mxq(W, 0)
    A = 1.0 / (1.0 + np.exp(-(Z * f64(enc_gain))))
    C = A * f64(code_gain)
    R = mxq(C, 1) @ mxq(W, 1).T
    y = (R * f64(dec_gain) - X) * f64(V)
    Y = y
    words, scales = planes(Y)
    return y, words, scales

@@ -1,0 +1,456 @@
+from contextlib import ExitStack
+
+import concourse.mybir as mybir
+from concourse.masks import make_identity
+
+T, F, H = 1024, 2048, 1024
+FLOPS = 2 * 2 * T * F * H
+
+F32 = mybir.dt.float32
+BF16 = mybir.dt.bfloat16
+I32 = mybir.dt.int32
+U32 = mybir.dt.uint32
+U8 = mybir.dt.uint8
+FP8 = mybir.dt.float8_e4m3fn
+FP8X4 = mybir.dt.float8_e4m3fn_x4
+ALU = mybir.AluOpType
+ACT = mybir.ActivationFunctionType
+
+P = 128
+PACK = 4
+GROUP = P * PACK
+TG, FG, HG = T // GROUP, F // GROUP, H // GROUP
+SCALE_BLOCK = 128
+BANKS = 8
+NSTAGE = 6
+BANK0 = 4
+XLAG = 1
+SQ0 = 5
+SQ1 = 7
+VW = (0, 1, 2, 3, 4, 5, 6, 7)
+RY = {1: [0, 1], 2: [2], 3: [3], 4: [4], 5: [5], 6: [6]}
+QY = {2: [0], 3: [1, 2], 4: [3], 5: [4], 6: [5]}
+
+
+def tile_tied_autoencoder_error_b11_kernel(
+    tc, X, W_bytes, W_scale, enc_gain, code_gain, dec_gain, V, out_0, out_1, out_2
+):
+    nc = tc.nc
+    with ExitStack() as ctx:
+        sb = ctx.enter_context(tc.tile_pool(name="sb", bufs=1))
+        ps = ctx.enter_context(tc.psum_pool(name="ps", bufs=1))
+        ctx.enter_context(tc.manual_schedule())
+
+        def tiles(name, count, width, dtype):
+            return [sb.tile([P, width], dtype, name="%s%d" % (name, i), align_bytes=64) for i in range(count)]
+
+        ident = sb.tile([P, P], F32, name="ident")
+        w_scale = sb.tile([P, FG, PACK * H // SCALE_BLOCK], F32, name="w_scale")
+        enc_raw = sb.tile([P, HG, PACK], BF16, name="enc_raw")
+        enc = sb.tile([P, HG, PACK], F32, name="enc")
+        cod_raw = sb.tile([P, HG, PACK], BF16, name="cod_raw")
+        cod = sb.tile([P, HG, PACK], F32, name="cod")
+        dec = sb.tile([P, FG, PACK], BF16, name="dec")
+        warm = sb.tile([P, 2], F32, name="warm")
+        w_bytes = tiles("w_bytes", 4, PACK * GROUP, U8)
+        w_wide = tiles("w_wide", FG, HG * PACK * GROUP, BF16)
+        rows = tiles("rows", TG * FG, PACK * GROUP, BF16)
+        x_t = tiles("x_t", TG * FG, PACK * GROUP, BF16)
+        x_codes = tiles("x_codes", TG * FG, GROUP, U32)
+        x_scales = tiles("x_scales", TG * FG, GROUP, U8)
+        enc_codes = tiles("enc_codes", FG * HG, GROUP, U32)
+        enc_scales = tiles("enc_scales", FG * HG, GROUP, U8)
+        dec_codes = tiles("dec_codes", FG, GROUP, U32)
+        dec_codes = [dec_codes[fg] if hg == 0 else x_codes[fg] for fg in range(FG) for hg in range(HG)]
+        dec_scales = tiles("dec_scales", FG, GROUP, U8)
+        dec_scales = [dec_scales[fg] if hg == 0 else x_scales[fg] for fg in range(FG) for hg in range(HG)]
+        c_codes = tiles("c_codes", TG * HG, GROUP, U32)
+        c_scales = tiles("c_scales", TG * HG, GROUP, U8)
+        stage = tiles("stage", NSTAGE, PACK * GROUP, BF16)
+        act = tiles("act", 2, PACK * GROUP, F32)
+        diff = tiles("diff", 2, PACK * GROUP, F32)
+        act = {(0, 0): act[0], (1, 0): act[1], (1, 1): act[0]}
+        y_f32 = [w[:].bitcast(F32) for w in w_wide]
+        act[(0, 1)] = diff[1]
+        y_codes = tiles("y_codes", 2, GROUP, U32)
+        y_scales = tiles("y_scales", TG, F, U8)
+        banks = [ps.tile([P, GROUP], F32, name="bank%d" % i) for i in range(BANKS)]
+
+        taken = {"bank": BANK0, "stage": 0, "turn": 0}
+        held = {}
+
+        def take(kind, ring, key):
+            held[key] = ring[taken[kind] % len(ring)]
+            taken[kind] = taken[kind] + 1
+            return held[key]
+
+        def copy(engine, out, in_):
+            if engine == "vector":
+                nc.vector.tensor_copy(out=out, in_=in_)
+            else:
+                nc.scalar.copy(out=out, in_=in_)
+
+        def quantize(codes, scales, src):
+            nc.vector.quantize_mx(out=codes.bitcast(FP8X4), scales=scales, in_=src)
+
+        def block(ap, r, c):
+            return ap[r * GROUP : (r + 1) * GROUP, c * GROUP : (c + 1) * GROUP].rearrange("(p s) n -> p s n", s=PACK)
+
+        def slots(tile):
+            return tile[:].rearrange("p (s n) -> p s n", s=PACK)
+
+        def wide(fg, hg):
+            return w_wide[fg][:, hg * PACK * GROUP : (hg + 1) * PACK * GROUP]
+
+        def load_w(fg, hg):
+            nc.sync.dma_start(out=slots(w_bytes[fg]), in_=block(W_bytes, fg, hg))
+
+        def load_rows(src, tg, fg):
+            nc.sync.dma_start(out=slots(rows[tg * FG + fg]), in_=block(src, tg, fg))
+
+        def widen(fg, hg):
+            src = slots(w_bytes[fg])
+            dst = wide(fg, hg).rearrange("p (t u m e) -> p t m u e", t=PACK, u=2, e=2)
+            quads = SCALE_BLOCK // PACK
+            for t in range(PACK):
+                for j in range(GROUP // SCALE_BLOCK):
+                    col = t * (H // SCALE_BLOCK) + hg * (GROUP // SCALE_BLOCK) + j
+                    nc.vector.tensor_scalar(
+                        out=dst[:, t, j * quads : (j + 1) * quads],
+                        in0=src[:, t, j * SCALE_BLOCK : (j + 1) * SCALE_BLOCK]
+                        .bitcast(FP8)
+                        .rearrange("p (q u e) -> p q u e", u=2, e=2),
+                        scalar1=w_scale[:, fg, col : col + 1],
+                        scalar2=None,
+                        op0=ALU.mult,
+                    )
+
+        def weave_w(fg, hg, u, engine):
+            dst = take("stage", stage, ("enc", fg, hg)) if u == 0 else held[("enc", fg, hg)]
+            copy(
+                engine,
+                dst[:].rearrange("p (u e c i t) -> p u c t e i", u=2, e=2, i=2, t=PACK)[:, u],
+                wide(fg, hg).rearrange("p (t u c i e) -> p u c t e i", t=PACK, u=2, i=2, e=2)[:, u],
+            )
+
+        def quantize_enc(fg, hg):
+            i = fg * HG + hg
+            quantize(enc_codes[i][:], enc_scales[i][:], held[("enc", fg, hg)][:])
+
+        def turn_x(tg, fg):
+            words = slots(rows[tg * FG + fg]).bitcast(F32)
+            for half in range(2):
+                bank = take("turn", banks[PACK:], ("x", tg, fg, half))
+                for s in range(2):
+                    for u in range(2):
+                        c = (2 * s + u) * P
+                        nc.tensor.transpose(bank[:, c : c + P], words[:, 2 * half + s, u : GROUP // 2 : 2], ident[:])
+
+        def empty_turned(key, dst, half, engine):
+            copy(
+                engine,
+                dst[:].bitcast(F32).rearrange("p (h s r u) -> p h s r u", h=2, s=2, u=2)[:, half],
+                held[key][:].rearrange("p (s u r) -> p s r u", s=2, u=2),
+            )
+
+        def empty_x(tg, fg, half, engine):
+            empty_turned(("x", tg, fg, half), x_t[tg * FG + fg], half, engine)
+
+        def quantize_x(tg, fg):
+            i = tg * FG + fg
+            quantize(x_codes[i][:], x_scales[i][:], x_t[i][:])
+
+        def encode(tg, hg, s, fg, first_bank=None):
+            if first_bank is not None:
+                held[("z", tg, hg, s)] = banks[first_bank + s]
+            elif fg == 0:
+                take("bank", banks, ("z", tg, hg, s))
+            bank = held[("z", tg, hg, s)]
+            cols = slice(s * P, (s + 1) * P)
+            nc.tensor.matmul_mx(
+                out=bank[:],
+                lhsT=enc_codes[fg * HG + hg][:, cols].bitcast(FP8X4),
+                lhsT_scale=enc_scales[fg * HG + hg][:, cols],
+                rhs=x_codes[tg * FG + fg][:].bitcast(FP8X4),
+                rhs_scale=x_scales[tg * FG + fg][:],
+                start=(fg == 0),
+                stop=(fg == FG - 1),
+            )
+
+        def squash(tg, hg, s, part=slice(0, GROUP)):
+            nc.scalar.activation(
+                out=slots(act[(tg, hg)])[:, s, part],
+                in_=held[("z", tg, hg, s)][:, part],
+                func=ACT.Sigmoid,
+                scale=enc[:, hg, s : s + 1],
+            )
+
+        def scale_code(tg, hg, s):
+            flat = take("stage", stage, ("flat", tg, hg)) if s == 0 else held[("flat", tg, hg)]
+            nc.scalar.activation(
+                out=slots(flat)[:, s], in_=slots(act[(tg, hg)])[:, s], func=ACT.Copy, scale=cod[:, hg, s : s + 1]
+            )
+
+        def weave_code(tg, hg, engine):
+            dst = take("stage", stage, ("c", tg, hg))
+            copy(
+                engine,
+                dst[:].rearrange("p (c i s) -> p c s i", i=4, s=PACK),
+                held[("flat", tg, hg)][:].rearrange("p (s c i) -> p c s i", s=PACK, i=4),
+            )
+
+        def make_code(tg, hg, half):
+            dst = take("stage", stage, ("c", tg, hg)) if half == 0 else held[("c", tg, hg)]
+            quads = GROUP // PACK // 2
+            part = slice(half * quads, (half + 1) * quads)
+            nc.vector.tensor_tensor(
+                out=dst[:].rearrange("p (c i s) -> p c s i", i=4, s=PACK)[:, part],
+                in0=act[(tg, hg)][:].rearrange("p (s c i) -> p c s i", s=PACK, i=4)[:, part],
+                in1=cod[:, hg].unsqueeze(1).unsqueeze(3).to_broadcast([P, quads, PACK, 4]),
+                op=ALU.mult,
+            )
+
+        def quantize_c(tg, hg):
+            i = tg * HG + hg
+            quantize(c_codes[i][:], c_scales[i][:], held[("c", tg, hg)][:])
+
+        def turn_w(fg, hg):
+            words = wide(fg, hg).bitcast(F32)
+            for half in range(2):
+                bank = take("turn", banks[PACK:], ("w", fg, hg, half)) if hg == 0 else take("bank", banks, ("w", fg, hg, half))
+                for c in range(0, GROUP, P):
+                    w0 = half * GROUP + c
+                    nc.tensor.transpose(bank[:, c : c + P], words[:, w0 : w0 + P], ident[:])
+
+        def empty_w(fg, hg, half, engine):
+            dst = take("stage", stage, ("dec", fg, hg)) if half == 0 else held[("dec", fg, hg)]
+            empty_turned(("w", fg, hg, half), dst, half, engine)
+
+        def quantize_dec(fg, hg):
+            i = fg * HG + hg
+            quantize(dec_codes[i][:], dec_scales[i][:], held[("dec", fg, hg)][:])
+
+        def decode(k, t):
+            tg, fg = divmod(k, FG)
+            bank = take("bank", banks, ("r", k, t))
+            cols = slice(t * P, (t + 1) * P)
+            for hg in range(HG):
+                nc.tensor.matmul_mx(
+                    out=bank[:],
+                    lhsT=dec_codes[fg * HG + hg][:, cols].bitcast(FP8X4),
+                    lhsT_scale=dec_scales[fg * HG + hg][:, cols],
+                    rhs=c_codes[tg * HG + hg][:].bitcast(FP8X4),
+                    rhs_scale=c_scales[tg * HG + hg][:],
+                    start=(hg == 0),
+                    stop=(hg == HG - 1),
+                )
+
+        def subtract(k, t):
+            nc.vector.scalar_tensor_tensor(
+                out=slots(diff[k % 2])[:, t],
+                in0=held[("r", k, t)][:],
+                scalar=dec[:, k % FG, t : t + 1],
+                in1=x_t[k][:].rearrange("p (n t) -> p t n", t=PACK)[:, t],
+                op0=ALU.mult,
+                op1=ALU.subtract,
+            )
+
+        def turn_d(k, s):
+            bank = take("bank", banks, ("d", k, s))
+            for t in range(PACK):
+                nc.tensor.transpose(
+                    bank[:, t * P : (t + 1) * P], slots(diff[k % 2])[:, t, s * P : (s + 1) * P], ident[:]
+                )
+
+        def y_part(k, part, parts):
+            width = PACK * GROUP // parts
+            return y_f32[k % FG][:, part * width : (part + 1) * width]
+
+        def weigh(k, s, part=0, parts=1):
+            ms = slice(part * P // parts, (part + 1) * P // parts)
+            nc.vector.tensor_tensor(
+                out=y_part(k, part, parts).rearrange("p (s m t) -> p s m t", s=PACK, t=PACK)[:, s],
+                in0=held[("d", k, s)][:].rearrange("p (t m) -> p m t", t=PACK)[:, ms],
+                in1=slots(rows[k])[:, s].rearrange("p (m t) -> p m t", t=PACK)[:, ms],
+                op=ALU.mult,
+            )
+
+        def store_y(k, part=0, parts=1):
+            tg, fg = divmod(k, FG)
+            cols = slice(part * GROUP // parts, (part + 1) * GROUP // parts)
+            nc.sync.dma_start(
+                out=block(out_0, tg, fg)[:, :, cols], in_=y_part(k, part, parts).rearrange("p (s n) -> p s n", s=PACK)
+            )
+
+        def round_y(k, engine, part=0, parts=1):
+            dst = take("stage", stage, ("y", k)) if part == 0 else held[("y", k)]
+            width = PACK * GROUP // parts
+            copy(
+                engine,
+                dst[:, part * width : (part + 1) * width].rearrange("p (c i s) -> p c s i", i=4, s=PACK),
+                y_part(k, part, parts).rearrange("p (s c i) -> p c s i", s=PACK, i=4),
+            )
+
+        def quantize_y(k, c0=0, c1=GROUP):
+            tg, fg = divmod(k, FG)
+            cols = slice(fg * GROUP + c0, fg * GROUP + c1)
+            quantize(y_codes[k % 2][:, c0:c1], y_scales[tg][:, cols], held[("y", k)][:, PACK * c0 : PACK * c1])
+            nc.sync.dma_start(
+                out=out_1[tg, :, cols, :].rearrange("p m t -> p (m t)").bitcast(I32),
+                in_=y_codes[k % 2][:, c0:c1].bitcast(I32),
+            )
+
+        def store_scales(tg, c0, c1, queues):
+            for q in range(4):
+                queues[q % len(queues)].dma_start(
+                    out=out_2[tg, 4 * q : 4 * q + 4, c0:c1].bitcast(I32),
+                    in_=y_scales[tg][32 * q : 32 * q + 4, c0:c1].bitcast(I32),
+                )
+
+        def load_gain(dst, src):
+            nc.sync.dma_start(out=dst[:], in_=src.rearrange("o (g p t) -> p (o g) t", p=P, t=PACK))
+
+
+        nc.scalar.dma_start(out=w_scale[:], in_=W_scale.rearrange("(g p t) j -> p g (t j)", p=P, t=PACK))
+        make_identity(nc, ident[:])
+        nc.vector.memset(warm[:, 0:1], 0.0)
+        nc.scalar.activation(out=warm[:, 1:2], in_=warm[:, 0:1], func=ACT.Sigmoid)
+        load_w(0, 0)
+        load_w(1, 0)
+        load_rows(X, 0, 0)
+        load_w(2, 0)
+        load_rows(X, 0, 1)
+        load_rows(X, 1, 0)
+        load_w(3, 0)
+        load_rows(X, 0, 2)
+        steps = [(fg, hg) for hg in range(HG) for fg in range(FG)]
+        widen(0, 0)
+        load_w(0, 1)
+        load_rows(X, 1, 1)
+        load_rows(X, 0, 3)
+        load_rows(X, 1, 2)
+        load_gain(enc_raw, enc_gain)
+        load_gain(cod_raw, code_gain)
+        load_gain(dec, dec_gain)
+
+        def x_blocks(i):
+            return [(tg, i - tg * XLAG) for tg in range(TG) if 0 <= i - tg * XLAG < FG]
+
+        for i, (fg, hg) in enumerate(steps):
+            if i + 1 < len(steps):
+                widen(*steps[i + 1])
+                if i + 1 < FG:
+                    load_w(i + 1, 1)
+                if i == 0:
+                    load_rows(X, 1, FG - 1)
+            for n, blk in enumerate(x_blocks(i)):
+                turn_x(*blk)
+                if n == 0 and 2 <= i <= FG:
+                    for s in range(2, PACK):
+                        encode(0, 0, s, i - 2, 0)
+            if i == SQ0:
+                nc.scalar.copy(out=enc[:], in_=enc_raw[:])
+                nc.scalar.copy(out=cod[:], in_=cod_raw[:])
+                for s in range(PACK):
+                    squash(0, 0, s)
+            weave_w(fg, hg, 0, "scalar")
+            weave_w(fg, hg, 1, "vector" if i in VW else "scalar")
+            for blk in x_blocks(i):
+                empty_x(*blk, 0, "scalar")
+                empty_x(*blk, 1, "scalar")
+            if i < FG:
+                turn_w(i, 0)
+                empty_w(i, 0, 0, "scalar")
+                empty_w(i, 0, 1, "scalar")
+            if i > 0:
+                quantize_enc(*steps[i - 1])
+                for blk in x_blocks(i - 1):
+                    quantize_x(*blk)
+                if i <= FG:
+                    quantize_dec(i - 1, 0)
+                    for s in range(2 if i < FG else PACK):
+                        encode(0, 0, s, i - 1, 0)
+            if i == FG:
+                for g in range(FG - 1):
+                    for s in range(PACK):
+                        encode(1, 0, s, g, PACK)
+            if i == FG + 1:
+                for s in range(PACK):
+                    encode(1, 0, s, FG - 1, PACK)
+            if i > FG:
+                for s in range(PACK):
+                    encode(0, 1, s, i - 1 - FG, 0)
+            if i == SQ1:
+                for s in range(PACK):
+                    squash(1, 0, s)
+        for k in range(TG * FG):
+            load_rows(V, *divmod(k, FG))
+        quantize_enc(FG - 1, 1)
+        for s in range(PACK):
+            encode(0, 1, s, FG - 1, 0)
+        make_code(0, 0, 0)
+        make_code(0, 0, 1)
+        for half in range(2):
+            for s in range(PACK):
+                squash(0, 1, s, slice(half * 256, half * 256 + 256))
+        for fg in range(2):
+            turn_w(fg, 1)
+            empty_w(fg, 1, 0, "scalar")
+            empty_w(fg, 1, 1, "scalar")
+        for s in range(PACK):
+            for fg in range(FG):
+                encode(1, 1, s, fg)
+        make_code(0, 1, 0)
+        quantize_c(0, 0)
+        make_code(0, 1, 1)
+        for s in range(PACK):
+            squash(1, 1, s)
+        quantize_dec(0, 1)
+        quantize_c(0, 1)
+        quantize_dec(1, 1)
+        units = TG * FG
+        for k in range(-1, units):
+            last = k + 1 == units
+            for pair in range(2):
+                two = range(2 * pair, 2 * pair + 2)
+                if not last:
+                    for t in two:
+                        decode(k + 1, t)
+                        subtract(k + 1, t)
+                if pair == 0 and 0 <= k < FG - 2:
+                    turn_w(k + 2, 1)
+                    empty_w(k + 2, 1, 0, "scalar")
+                    empty_w(k + 2, 1, 1, "scalar")
+                if pair == 1:
+                    if k in (1, 2):
+                        quantize_c(1, k - 1)
+                    if 0 <= k < FG - 2:
+                        quantize_dec(k + 2, 1)
+                    for j in QY.get(k, []):
+                        quantize_y(j)
+                        if j == FG - 1:
+                            store_scales(0, 0, F, [nc.sync])
+                if k >= 0:
+                    for s in two:
+                        turn_d(k, s)
+                        if not last:
+                            weigh(k, s)
+            if 0 <= k and not last:
+                store_y(k)
+            if k in (-1, 0):
+                for s in range(PACK):
+                    scale_code(1, k + 1, s)
+                weave_code(1, k + 1, "scalar")
+            for j in RY.get(k, []):
+                round_y(j, "scalar")
+        k = units - 1
+        for half in range(2):
+            for s in range(PACK):
+                weigh(k, s, half, 2)
+            store_y(k, half, 2)
+            round_y(k, "scalar" if half == 0 else "vector", half, 2)
+        quantize_y(k - 1)
+        store_scales(1, 0, F - GROUP, [nc.sync])
+        quantize_y(k, 0, 256)
+        quantize_y(k, 256, 512)
+        store_scales(1, F - GROUP, F, [nc.scalar, nc.sync])

@@ -25,11 +25,21 @@ BANKS = 8
 NSTAGE = 6
 BANK0 = 4
 XLAG = 1
+EW = 4
 SQ0 = 5
 SQ1 = 7
 VW = (0, 1, 2, 3, 4, 5, 6, 7)
-RY = {1: [0, 1], 2: [2], 3: [3], 4: [4], 5: [5], 6: [6]}
-QY = {2: [0], 3: [1, 2], 4: [3], 5: [4], 6: [5]}
+RY = {1: [0, 1], 2: [2], 3: [3], 4: [4], 5: [5]}
+QY = {2: [0], 3: [1, 2], 4: [3], 5: [4]}
+FIRST = [("w", 0, 0), ("w", 1, 0), ("x", 0, 0), ("w", 2, 0), ("x", 0, 1), ("x", 1, 0), ("w", 3, 0), ("x", 0, 2)]
+MID = [(1, 1), (0, 3), (1, 2)]
+LATE = [(1, 3)]
+ADD0 = 3
+ADDT = 1
+QD = 4
+VW0 = ()
+SPLIT = 1
+ADD1 = 7
 
 
 def tile_tied_autoencoder_error_b11_kernel(
@@ -50,7 +60,8 @@ def tile_tied_autoencoder_error_b11_kernel(
         enc = sb.tile([P, HG, PACK], F32, name="enc")
         cod_raw = sb.tile([P, HG, PACK], BF16, name="cod_raw")
         cod = sb.tile([P, HG, PACK], F32, name="cod")
-        dec = sb.tile([P, FG, PACK], BF16, name="dec")
+        dec_raw = sb.tile([P, FG, PACK], BF16, name="dec_raw")
+        dec = sb.tile([P, FG, PACK], F32, name="dec")
         warm = sb.tile([P, 2], F32, name="warm")
         w_bytes = tiles("w_bytes", 4, PACK * GROUP, U8)
         w_wide = tiles("w_wide", FG, HG * PACK * GROUP, BF16)
@@ -72,6 +83,7 @@ def tile_tied_autoencoder_error_b11_kernel(
         act = {(0, 0): act[0], (1, 0): act[1], (1, 1): act[0]}
         y_f32 = [w[:].bitcast(F32) for w in w_wide]
         act[(0, 1)] = diff[1]
+        minus_x = tiles("minus_x", 2, GROUP, F32)
         y_codes = tiles("y_codes", 2, GROUP, U32)
         y_scales = tiles("y_scales", TG, F, U8)
         banks = [ps.tile([P, GROUP], F32, name="bank%d" % i) for i in range(BANKS)]
@@ -245,7 +257,23 @@ def tile_tied_autoencoder_error_b11_kernel(
                     stop=(hg == HG - 1),
                 )
 
+        def on_tensor(k, t):
+            return ADD0 <= k < ADD1 and t == ADDT
+
+        def negate_x(k):
+            nc.scalar.activation(
+                out=minus_x[k % 2][:],
+                in_=x_t[k][:].rearrange("p (n t) -> p t n", t=PACK)[:, ADDT],
+                func=ACT.Copy,
+                scale=-1.0,
+            )
+
         def subtract(k, t):
+            if on_tensor(k, t):
+                nc.scalar.activation(
+                    out=slots(diff[k % 2])[:, t], in_=held[("r", k, t)][:], func=ACT.Copy, scale=dec[:, k % FG, t : t + 1]
+                )
+                return
             nc.vector.scalar_tensor_tensor(
                 out=slots(diff[k % 2])[:, t],
                 in0=held[("r", k, t)][:],
@@ -258,9 +286,16 @@ def tile_tied_autoencoder_error_b11_kernel(
         def turn_d(k, s):
             bank = take("bank", banks, ("d", k, s))
             for t in range(PACK):
-                nc.tensor.transpose(
-                    bank[:, t * P : (t + 1) * P], slots(diff[k % 2])[:, t, s * P : (s + 1) * P], ident[:]
-                )
+                terms = [slots(diff[k % 2])[:, t]] + ([minus_x[k % 2][:]] if on_tensor(k, t) else [])
+                for n, term in enumerate(terms):
+                    nc.tensor.matmul(
+                        bank[:, t * P : (t + 1) * P],
+                        lhsT=term[:, s * P : (s + 1) * P],
+                        rhs=ident[:],
+                        start=(n == 0),
+                        stop=(n == len(terms) - 1),
+                        is_transpose=True,
+                    )
 
         def y_part(k, part, parts):
             width = PACK * GROUP // parts
@@ -315,23 +350,19 @@ def tile_tied_autoencoder_error_b11_kernel(
         make_identity(nc, ident[:])
         nc.vector.memset(warm[:, 0:1], 0.0)
         nc.scalar.activation(out=warm[:, 1:2], in_=warm[:, 0:1], func=ACT.Sigmoid)
-        load_w(0, 0)
-        load_w(1, 0)
-        load_rows(X, 0, 0)
-        load_w(2, 0)
-        load_rows(X, 0, 1)
-        load_rows(X, 1, 0)
-        load_w(3, 0)
-        load_rows(X, 0, 2)
+        for kind, a, b in FIRST:
+            if kind == "w":
+                load_w(a, b)
+            else:
+                load_rows(X, a, b)
         steps = [(fg, hg) for hg in range(HG) for fg in range(FG)]
         widen(0, 0)
         load_w(0, 1)
-        load_rows(X, 1, 1)
-        load_rows(X, 0, 3)
-        load_rows(X, 1, 2)
+        for blk in MID:
+            load_rows(X, *blk)
         load_gain(enc_raw, enc_gain)
         load_gain(cod_raw, code_gain)
-        load_gain(dec, dec_gain)
+        load_gain(dec_raw, dec_gain)
 
         def x_blocks(i):
             return [(tg, i - tg * XLAG) for tg in range(TG) if 0 <= i - tg * XLAG < FG]
@@ -342,23 +373,25 @@ def tile_tied_autoencoder_error_b11_kernel(
                 if i + 1 < FG:
                     load_w(i + 1, 1)
                 if i == 0:
-                    load_rows(X, 1, FG - 1)
+                    for blk in LATE:
+                        load_rows(X, *blk)
             for n, blk in enumerate(x_blocks(i)):
                 turn_x(*blk)
-                if n == 0 and 2 <= i <= FG:
+                if n == 0 and 2 <= i <= FG and SPLIT:
                     for s in range(2, PACK):
                         encode(0, 0, s, i - 2, 0)
             if i == SQ0:
                 nc.scalar.copy(out=enc[:], in_=enc_raw[:])
                 nc.scalar.copy(out=cod[:], in_=cod_raw[:])
+                nc.scalar.copy(out=dec[:], in_=dec_raw[:])
                 for s in range(PACK):
                     squash(0, 0, s)
-            weave_w(fg, hg, 0, "scalar")
+            weave_w(fg, hg, 0, "vector" if i in VW0 else "scalar")
             weave_w(fg, hg, 1, "vector" if i in VW else "scalar")
             for blk in x_blocks(i):
                 empty_x(*blk, 0, "scalar")
                 empty_x(*blk, 1, "scalar")
-            if i < FG:
+            if i < EW:
                 turn_w(i, 0)
                 empty_w(i, 0, 0, "scalar")
                 empty_w(i, 0, 1, "scalar")
@@ -366,15 +399,16 @@ def tile_tied_autoencoder_error_b11_kernel(
                 quantize_enc(*steps[i - 1])
                 for blk in x_blocks(i - 1):
                     quantize_x(*blk)
-                if i <= FG:
+                if i <= QD:
                     quantize_dec(i - 1, 0)
-                    for s in range(2 if i < FG else PACK):
+                if i <= FG:
+                    for s in range(2 if i < FG and SPLIT else PACK):
                         encode(0, 0, s, i - 1, 0)
             if i == FG:
-                for g in range(FG - 1):
+                for g in range(FG - XLAG):
                     for s in range(PACK):
                         encode(1, 0, s, g, PACK)
-            if i == FG + 1:
+            if i == FG + 1 and XLAG:
                 for s in range(PACK):
                     encode(1, 0, s, FG - 1, PACK)
             if i > FG:
@@ -390,6 +424,8 @@ def tile_tied_autoencoder_error_b11_kernel(
             encode(0, 1, s, FG - 1, 0)
         make_code(0, 0, 0)
         make_code(0, 0, 1)
+        for fg in range(QD, FG):
+            quantize_dec(fg, 0)
         for half in range(2):
             for s in range(PACK):
                 squash(0, 1, s, slice(half * 256, half * 256 + 256))
@@ -409,7 +445,7 @@ def tile_tied_autoencoder_error_b11_kernel(
         quantize_c(0, 1)
         quantize_dec(1, 1)
         units = TG * FG
-        for k in range(-1, units):
+        for k in range(-1, units - 2):
             last = k + 1 == units
             for pair in range(2):
                 two = range(2 * pair, 2 * pair + 2)
@@ -418,14 +454,16 @@ def tile_tied_autoencoder_error_b11_kernel(
                         decode(k + 1, t)
                         subtract(k + 1, t)
                 if pair == 0 and 0 <= k < FG - 2:
-                    turn_w(k + 2, 1)
-                    empty_w(k + 2, 1, 0, "scalar")
-                    empty_w(k + 2, 1, 1, "scalar")
+                    for hg in range(0 if k + 2 >= EW else 1, HG):
+                        turn_w(k + 2, hg)
+                        empty_w(k + 2, hg, 0, "scalar")
+                        empty_w(k + 2, hg, 1, "scalar")
                 if pair == 1:
                     if k in (1, 2):
                         quantize_c(1, k - 1)
                     if 0 <= k < FG - 2:
-                        quantize_dec(k + 2, 1)
+                        for hg in range(0 if k + 2 >= EW else 1, HG):
+                            quantize_dec(k + 2, hg)
                     for j in QY.get(k, []):
                         quantize_y(j)
                         if j == FG - 1:
@@ -441,16 +479,39 @@ def tile_tied_autoencoder_error_b11_kernel(
                 for s in range(PACK):
                     scale_code(1, k + 1, s)
                 weave_code(1, k + 1, "scalar")
+            if ADD0 <= k + 2 < ADD1:
+                negate_x(k + 2)
             for j in RY.get(k, []):
                 round_y(j, "scalar")
         k = units - 1
-        for half in range(2):
-            for s in range(PACK):
-                weigh(k, s, half, 2)
-            store_y(k, half, 2)
-            round_y(k, "scalar" if half == 0 else "vector", half, 2)
+        for t in range(2):
+            decode(k, t)
+            subtract(k, t)
+        for s in range(2):
+            turn_d(k - 1, s)
+            weigh(k - 1, s)
+        for t in range(2, PACK):
+            decode(k, t)
+        for s in range(2, PACK):
+            turn_d(k - 1, s)
+            weigh(k - 1, s)
+        store_y(k - 1)
+        round_y(k - 1, "scalar")
+        for t in range(2, PACK):
+            subtract(k, t)
+        quantize_y(k - 2)
+        store_scales(1, 0, F // 2, [nc.sync])
+        for s in range(PACK):
+            turn_d(k, s)
+        for s in range(PACK):
+            weigh(k, s, 0, 2)
+        store_y(k, 0, 2)
+        round_y(k, "scalar", 0, 2)
         quantize_y(k - 1)
-        store_scales(1, 0, F - GROUP, [nc.sync])
+        for s in range(PACK):
+            weigh(k, s, 1, 2)
+        store_y(k, 1, 2)
         quantize_y(k, 0, 256)
+        round_y(k, "vector", 1, 2)
         quantize_y(k, 256, 512)
-        store_scales(1, F - GROUP, F, [nc.scalar, nc.sync])
+        store_scales(1, F // 2, F, [nc.scalar, nc.sync])

@@ -29,17 +29,20 @@ EW = 4
 SQ0 = 5
 SQ1 = 7
 VW = (0, 1, 2, 3, 4, 5, 6, 7)
-RY = {1: [0, 1], 2: [2], 3: [3], 4: [4], 5: [5]}
-QY = {2: [0], 3: [1, 2], 4: [3], 5: [4]}
-FIRST = [("w", 0, 0), ("w", 1, 0), ("x", 0, 0), ("w", 2, 0), ("x", 0, 1), ("x", 1, 0), ("w", 3, 0), ("x", 0, 2)]
+RY = {1: [0, 1], 2: [2], 3: [3], 4: [4], 5: [5], 6: [6]}
+QY = {2: [0], 3: [1, 2], 4: [3], 5: [4], 6: [5]}
+FIRST = [("w", 0, 0), ("x", 0, 0), ("w", 1, 0), ("x", 0, 1), ("w", 2, 0), ("x", 1, 0), ("w", 3, 0), ("x", 0, 2)]
 MID = [(1, 1), (0, 3), (1, 2)]
 LATE = [(1, 3)]
 ADD0 = 3
 ADDT = 1
+ADD1 = 8
 QD = 4
 VW0 = ()
 SPLIT = 1
-ADD1 = 7
+WW = (0, 0, 0, 0)
+WX = {}
+WFIRST = 1
 
 
 def tile_tied_autoencoder_error_b11_kernel(
@@ -149,10 +152,12 @@ def tile_tied_autoencoder_error_b11_kernel(
             i = fg * HG + hg
             quantize(enc_codes[i][:], enc_scales[i][:], held[("enc", fg, hg)][:])
 
-        def turn_x(tg, fg):
+        def turn_x(tg, fg, warm_passes=0):
             words = slots(rows[tg * FG + fg]).bitcast(F32)
             for half in range(2):
                 bank = take("turn", banks[PACK:], ("x", tg, fg, half))
+                if half == 0:
+                    keep_warm(bank, warm_passes)
                 for s in range(2):
                     for u in range(2):
                         c = (2 * s + u) * P
@@ -226,10 +231,24 @@ def tile_tied_autoencoder_error_b11_kernel(
             i = tg * HG + hg
             quantize(c_codes[i][:], c_scales[i][:], held[("c", tg, hg)][:])
 
-        def turn_w(fg, hg):
+        def keep_warm(bank, passes):
+            for n in range(passes):
+                nc.tensor.matmul_mx(
+                    out=bank[:],
+                    lhsT=enc_codes[0][:, :P].bitcast(FP8X4),
+                    lhsT_scale=enc_scales[0][:, :P],
+                    rhs=enc_codes[0][:].bitcast(FP8X4),
+                    rhs_scale=enc_scales[0][:],
+                    start=True,
+                    stop=True,
+                )
+
+        def turn_w(fg, hg, warm_passes=0):
             words = wide(fg, hg).bitcast(F32)
             for half in range(2):
                 bank = take("turn", banks[PACK:], ("w", fg, hg, half)) if hg == 0 else take("bank", banks, ("w", fg, hg, half))
+                if half == 0:
+                    keep_warm(bank, warm_passes)
                 for c in range(0, GROUP, P):
                     w0 = half * GROUP + c
                     nc.tensor.transpose(bank[:, c : c + P], words[:, w0 : w0 + P], ident[:])
@@ -317,6 +336,11 @@ def tile_tied_autoencoder_error_b11_kernel(
                 out=block(out_0, tg, fg)[:, :, cols], in_=y_part(k, part, parts).rearrange("p (s n) -> p s n", s=PACK)
             )
 
+        def store_rows(k, two):
+            tg, fg = divmod(k, FG)
+            rows_s = slice(two[0], two[-1] + 1)
+            nc.sync.dma_start(out=block(out_0, tg, fg)[:, rows_s], in_=slots(y_f32[k % FG])[:, rows_s])
+
         def round_y(k, engine, part=0, parts=1):
             dst = take("stage", stage, ("y", k)) if part == 0 else held[("y", k)]
             width = PACK * GROUP // parts
@@ -368,6 +392,13 @@ def tile_tied_autoencoder_error_b11_kernel(
             return [(tg, i - tg * XLAG) for tg in range(TG) if 0 <= i - tg * XLAG < FG]
 
         for i, (fg, hg) in enumerate(steps):
+            if i == 0:
+                weave_w(0, 0, 0, "scalar")
+                weave_w(0, 0, 1, "vector")
+                if WFIRST:
+                    turn_w(0, 0)
+                    empty_w(0, 0, 0, "scalar")
+                    empty_w(0, 0, 1, "scalar")
             if i + 1 < len(steps):
                 widen(*steps[i + 1])
                 if i + 1 < FG:
@@ -376,7 +407,7 @@ def tile_tied_autoencoder_error_b11_kernel(
                     for blk in LATE:
                         load_rows(X, *blk)
             for n, blk in enumerate(x_blocks(i)):
-                turn_x(*blk)
+                turn_x(*blk, WX.get(blk, 0))
                 if n == 0 and 2 <= i <= FG and SPLIT:
                     for s in range(2, PACK):
                         encode(0, 0, s, i - 2, 0)
@@ -386,17 +417,21 @@ def tile_tied_autoencoder_error_b11_kernel(
                 nc.scalar.copy(out=dec[:], in_=dec_raw[:])
                 for s in range(PACK):
                     squash(0, 0, s)
-            weave_w(fg, hg, 0, "vector" if i in VW0 else "scalar")
-            weave_w(fg, hg, 1, "vector" if i in VW else "scalar")
+            if i > 0:
+                weave_w(fg, hg, 0, "vector" if i in VW0 else "scalar")
+                weave_w(fg, hg, 1, "vector" if i in VW else "scalar")
             for blk in x_blocks(i):
                 empty_x(*blk, 0, "scalar")
                 empty_x(*blk, 1, "scalar")
-            if i < EW:
-                turn_w(i, 0)
+            if WFIRST <= i < EW:
+                turn_w(i, 0, WW[i])
                 empty_w(i, 0, 0, "scalar")
                 empty_w(i, 0, 1, "scalar")
-            if i > 0:
+            if i == 0:
+                quantize_enc(0, 0)
+            if i > 1:
                 quantize_enc(*steps[i - 1])
+            if i > 0:
                 for blk in x_blocks(i - 1):
                     quantize_x(*blk)
                 if i <= QD:
@@ -445,7 +480,7 @@ def tile_tied_autoencoder_error_b11_kernel(
         quantize_c(0, 1)
         quantize_dec(1, 1)
         units = TG * FG
-        for k in range(-1, units - 2):
+        for k in range(-1, units - 1):
             last = k + 1 == units
             for pair in range(2):
                 two = range(2 * pair, 2 * pair + 2)
@@ -473,8 +508,7 @@ def tile_tied_autoencoder_error_b11_kernel(
                         turn_d(k, s)
                         if not last:
                             weigh(k, s)
-            if 0 <= k and not last:
-                store_y(k)
+                    store_rows(k, two)
             if k in (-1, 0):
                 for s in range(PACK):
                     scale_code(1, k + 1, s)
@@ -484,34 +518,16 @@ def tile_tied_autoencoder_error_b11_kernel(
             for j in RY.get(k, []):
                 round_y(j, "scalar")
         k = units - 1
-        for t in range(2):
-            decode(k, t)
-            subtract(k, t)
-        for s in range(2):
-            turn_d(k - 1, s)
-            weigh(k - 1, s)
-        for t in range(2, PACK):
-            decode(k, t)
-        for s in range(2, PACK):
-            turn_d(k - 1, s)
-            weigh(k - 1, s)
-        store_y(k - 1)
-        round_y(k - 1, "scalar")
-        for t in range(2, PACK):
-            subtract(k, t)
-        quantize_y(k - 2)
         store_scales(1, 0, F // 2, [nc.sync])
         for s in range(PACK):
             turn_d(k, s)
-        for s in range(PACK):
-            weigh(k, s, 0, 2)
-        store_y(k, 0, 2)
+        for half in range(2):
+            for s in range(PACK):
+                weigh(k, s, half, 2)
+            store_y(k, half, 2)
         round_y(k, "scalar", 0, 2)
         quantize_y(k - 1)
-        for s in range(PACK):
-            weigh(k, s, 1, 2)
-        store_y(k, 1, 2)
-        quantize_y(k, 0, 256)
         round_y(k, "vector", 1, 2)
+        quantize_y(k, 0, 256)
         quantize_y(k, 256, 512)
         store_scales(1, F // 2, F, [nc.scalar, nc.sync])

from contextlib import ExitStack

import concourse.mybir as mybir
from concourse.masks import make_identity

T, F, H = 1024, 2048, 1024
FLOPS = 2 * 2 * T * F * H

F32 = mybir.dt.float32
BF16 = mybir.dt.bfloat16
I32 = mybir.dt.int32
U32 = mybir.dt.uint32
U8 = mybir.dt.uint8
FP8 = mybir.dt.float8_e4m3fn
FP8X4 = mybir.dt.float8_e4m3fn_x4
ALU = mybir.AluOpType
ACT = mybir.ActivationFunctionType

P = 128
PACK = 4
GROUP = P * PACK
TG, FG, HG = T // GROUP, F // GROUP, H // GROUP
SCALE_BLOCK = 128
BANKS = 8
NSTAGE = 6
BANK0 = 4
XLAG = 1
EW = 4
SQ0 = 5
SQ1 = 7
VW = (0, 1, 2, 3, 4, 5, 6, 7)
RY = {1: [0, 1], 2: [2], 3: [3], 4: [4], 5: [5], 6: [6]}
QY = {2: [0], 3: [1, 2], 4: [3], 5: [4], 6: [5]}
FIRST = [("w", 0, 0), ("x", 0, 0), ("w", 1, 0), ("x", 0, 1), ("w", 2, 0), ("x", 1, 0), ("w", 3, 0), ("x", 0, 2)]
MID = [(1, 1), (0, 3), (1, 2)]
LATE = [(1, 3)]
ADD0 = 3
ADDT = 1
ADD1 = 8
QD = 4
VW0 = ()
SPLIT = 1
WW = (0, 0, 0, 0)
WX = {}
WFIRST = 1


def tile_tied_autoencoder_error_b11_kernel(
    tc, X, W_bytes, W_scale, enc_gain, code_gain, dec_gain, V, out_0, out_1, out_2
):
    nc = tc.nc
    with ExitStack() as ctx:
        sb = ctx.enter_context(tc.tile_pool(name="sb", bufs=1))
        ps = ctx.enter_context(tc.psum_pool(name="ps", bufs=1))
        ctx.enter_context(tc.manual_schedule())

        def tiles(name, count, width, dtype):
            return [sb.tile([P, width], dtype, name="%s%d" % (name, i), align_bytes=64) for i in range(count)]

        ident = sb.tile([P, P], F32, name="ident")
        w_scale = sb.tile([P, FG, PACK * H // SCALE_BLOCK], F32, name="w_scale")
        enc_raw = sb.tile([P, HG, PACK], BF16, name="enc_raw")
        enc = sb.tile([P, HG, PACK], F32, name="enc")
        cod_raw = sb.tile([P, HG, PACK], BF16, name="cod_raw")
        cod = sb.tile([P, HG, PACK], F32, name="cod")
        dec_raw = sb.tile([P, FG, PACK], BF16, name="dec_raw")
        dec = sb.tile([P, FG, PACK], F32, name="dec")
        warm = sb.tile([P, 2], F32, name="warm")
        w_bytes = tiles("w_bytes", 4, PACK * GROUP, U8)
        w_wide = tiles("w_wide", FG, HG * PACK * GROUP, BF16)
        rows = tiles("rows", TG * FG, PACK * GROUP, BF16)
        x_t = tiles("x_t", TG * FG, PACK * GROUP, BF16)
        x_codes = tiles("x_codes", TG * FG, GROUP, U32)
        x_scales = tiles("x_scales", TG * FG, GROUP, U8)
        enc_codes = tiles("enc_codes", FG * HG, GROUP, U32)
        enc_scales = tiles("enc_scales", FG * HG, GROUP, U8)
        dec_codes = tiles("dec_codes", FG, GROUP, U32)
        dec_codes = [dec_codes[fg] if hg == 0 else x_codes[fg] for fg in range(FG) for hg in range(HG)]
        dec_scales = tiles("dec_scales", FG, GROUP, U8)
        dec_scales = [dec_scales[fg] if hg == 0 else x_scales[fg] for fg in range(FG) for hg in range(HG)]
        c_codes = tiles("c_codes", TG * HG, GROUP, U32)
        c_scales = tiles("c_scales", TG * HG, GROUP, U8)
        stage = tiles("stage", NSTAGE, PACK * GROUP, BF16)
        act = tiles("act", 2, PACK * GROUP, F32)
        diff = tiles("diff", 2, PACK * GROUP, F32)
        act = {(0, 0): act[0], (1, 0): act[1], (1, 1): act[0]}
        y_f32 = [w[:].bitcast(F32) for w in w_wide]
        act[(0, 1)] = diff[1]
        minus_x = tiles("minus_x", 2, GROUP, F32)
        y_codes = tiles("y_codes", 2, GROUP, U32)
        y_scales = tiles("y_scales", TG, F, U8)
        banks = [ps.tile([P, GROUP], F32, name="bank%d" % i) for i in range(BANKS)]

        taken = {"bank": BANK0, "stage": 0, "turn": 0}
        held = {}

        def take(kind, ring, key):
            held[key] = ring[taken[kind] % len(ring)]
            taken[kind] = taken[kind] + 1
            return held[key]

        def copy(engine, out, in_):
            if engine == "vector":
                nc.vector.tensor_copy(out=out, in_=in_)
            else:
                nc.scalar.copy(out=out, in_=in_)

        def quantize(codes, scales, src):
            nc.vector.quantize_mx(out=codes.bitcast(FP8X4), scales=scales, in_=src)

        def block(ap, r, c):
            return ap[r * GROUP : (r + 1) * GROUP, c * GROUP : (c + 1) * GROUP].rearrange("(p s) n -> p s n", s=PACK)

        def slots(tile):
            return tile[:].rearrange("p (s n) -> p s n", s=PACK)

        def wide(fg, hg):
            return w_wide[fg][:, hg * PACK * GROUP : (hg + 1) * PACK * GROUP]

        def load_w(fg, hg):
            nc.sync.dma_start(out=slots(w_bytes[fg]), in_=block(W_bytes, fg, hg))

        def load_rows(src, tg, fg):
            nc.sync.dma_start(out=slots(rows[tg * FG + fg]), in_=block(src, tg, fg))

        def widen(fg, hg):
            src = slots(w_bytes[fg])
            dst = wide(fg, hg).rearrange("p (t u m e) -> p t m u e", t=PACK, u=2, e=2)
            quads = SCALE_BLOCK // PACK
            for t in range(PACK):
                for j in range(GROUP // SCALE_BLOCK):
                    col = t * (H // SCALE_BLOCK) + hg * (GROUP // SCALE_BLOCK) + j
                    nc.vector.tensor_scalar(
                        out=dst[:, t, j * quads : (j + 1) * quads],
                        in0=src[:, t, j * SCALE_BLOCK : (j + 1) * SCALE_BLOCK]
                        .bitcast(FP8)
                        .rearrange("p (q u e) -> p q u e", u=2, e=2),
                        scalar1=w_scale[:, fg, col : col + 1],
                        scalar2=None,
                        op0=ALU.mult,
                    )

        def weave_w(fg, hg, u, engine):
            dst = take("stage", stage, ("enc", fg, hg)) if u == 0 else held[("enc", fg, hg)]
            copy(
                engine,
                dst[:].rearrange("p (u e c i t) -> p u c t e i", u=2, e=2, i=2, t=PACK)[:, u],
                wide(fg, hg).rearrange("p (t u c i e) -> p u c t e i", t=PACK, u=2, i=2, e=2)[:, u],
            )

        def quantize_enc(fg, hg):
            i = fg * HG + hg
            quantize(enc_codes[i][:], enc_scales[i][:], held[("enc", fg, hg)][:])

        def turn_x(tg, fg, warm_passes=0):
            words = slots(rows[tg * FG + fg]).bitcast(F32)
            for half in range(2):
                bank = take("turn", banks[PACK:], ("x", tg, fg, half))
                if half == 0:
                    keep_warm(bank, warm_passes)
                for s in range(2):
                    for u in range(2):
                        c = (2 * s + u) * P
                        nc.tensor.transpose(bank[:, c : c + P], words[:, 2 * half + s, u : GROUP // 2 : 2], ident[:])

        def empty_turned(key, dst, half, engine):
            copy(
                engine,
                dst[:].bitcast(F32).rearrange("p (h s r u) -> p h s r u", h=2, s=2, u=2)[:, half],
                held[key][:].rearrange("p (s u r) -> p s r u", s=2, u=2),
            )

        def empty_x(tg, fg, half, engine):
            empty_turned(("x", tg, fg, half), x_t[tg * FG + fg], half, engine)

        def quantize_x(tg, fg):
            i = tg * FG + fg
            quantize(x_codes[i][:], x_scales[i][:], x_t[i][:])

        def encode(tg, hg, s, fg, first_bank=None):
            if first_bank is not None:
                held[("z", tg, hg, s)] = banks[first_bank + s]
            elif fg == 0:
                take("bank", banks, ("z", tg, hg, s))
            bank = held[("z", tg, hg, s)]
            cols = slice(s * P, (s + 1) * P)
            nc.tensor.matmul_mx(
                out=bank[:],
                lhsT=enc_codes[fg * HG + hg][:, cols].bitcast(FP8X4),
                lhsT_scale=enc_scales[fg * HG + hg][:, cols],
                rhs=x_codes[tg * FG + fg][:].bitcast(FP8X4),
                rhs_scale=x_scales[tg * FG + fg][:],
                start=(fg == 0),
                stop=(fg == FG - 1),
            )

        def squash(tg, hg, s, part=slice(0, GROUP)):
            nc.scalar.activation(
                out=slots(act[(tg, hg)])[:, s, part],
                in_=held[("z", tg, hg, s)][:, part],
                func=ACT.Sigmoid,
                scale=enc[:, hg, s : s + 1],
            )

        def scale_code(tg, hg, s):
            flat = take("stage", stage, ("flat", tg, hg)) if s == 0 else held[("flat", tg, hg)]
            nc.scalar.activation(
                out=slots(flat)[:, s], in_=slots(act[(tg, hg)])[:, s], func=ACT.Copy, scale=cod[:, hg, s : s + 1]
            )

        def weave_code(tg, hg, engine):
            dst = take("stage", stage, ("c", tg, hg))
            copy(
                engine,
                dst[:].rearrange("p (c i s) -> p c s i", i=4, s=PACK),
                held[("flat", tg, hg)][:].rearrange("p (s c i) -> p c s i", s=PACK, i=4),
            )

        def make_code(tg, hg, half):
            dst = take("stage", stage, ("c", tg, hg)) if half == 0 else held[("c", tg, hg)]
            quads = GROUP // PACK // 2
            part = slice(half * quads, (half + 1) * quads)
            nc.vector.tensor_tensor(
                out=dst[:].rearrange("p (c i s) -> p c s i", i=4, s=PACK)[:, part],
                in0=act[(tg, hg)][:].rearrange("p (s c i) -> p c s i", s=PACK, i=4)[:, part],
                in1=cod[:, hg].unsqueeze(1).unsqueeze(3).to_broadcast([P, quads, PACK, 4]),
                op=ALU.mult,
            )

        def quantize_c(tg, hg):
            i = tg * HG + hg
            quantize(c_codes[i][:], c_scales[i][:], held[("c", tg, hg)][:])

        def keep_warm(bank, passes):
            for n in range(passes):
                nc.tensor.matmul_mx(
                    out=bank[:],
                    lhsT=enc_codes[0][:, :P].bitcast(FP8X4),
                    lhsT_scale=enc_scales[0][:, :P],
                    rhs=enc_codes[0][:].bitcast(FP8X4),
                    rhs_scale=enc_scales[0][:],
                    start=True,
                    stop=True,
                )

        def turn_w(fg, hg, warm_passes=0):
            words = wide(fg, hg).bitcast(F32)
            for half in range(2):
                bank = take("turn", banks[PACK:], ("w", fg, hg, half)) if hg == 0 else take("bank", banks, ("w", fg, hg, half))
                if half == 0:
                    keep_warm(bank, warm_passes)
                for c in range(0, GROUP, P):
                    w0 = half * GROUP + c
                    nc.tensor.transpose(bank[:, c : c + P], words[:, w0 : w0 + P], ident[:])

        def empty_w(fg, hg, half, engine):
            dst = take("stage", stage, ("dec", fg, hg)) if half == 0 else held[("dec", fg, hg)]
            empty_turned(("w", fg, hg, half), dst, half, engine)

        def quantize_dec(fg, hg):
            i = fg * HG + hg
            quantize(dec_codes[i][:], dec_scales[i][:], held[("dec", fg, hg)][:])

        def decode(k, t):
            tg, fg = divmod(k, FG)
            bank = take("bank", banks, ("r", k, t))
            cols = slice(t * P, (t + 1) * P)
            for hg in range(HG):
                nc.tensor.matmul_mx(
                    out=bank[:],
                    lhsT=dec_codes[fg * HG + hg][:, cols].bitcast(FP8X4),
                    lhsT_scale=dec_scales[fg * HG + hg][:, cols],
                    rhs=c_codes[tg * HG + hg][:].bitcast(FP8X4),
                    rhs_scale=c_scales[tg * HG + hg][:],
                    start=(hg == 0),
                    stop=(hg == HG - 1),
                )

        def on_tensor(k, t):
            return ADD0 <= k < ADD1 and t == ADDT

        def negate_x(k):
            nc.scalar.activation(
                out=minus_x[k % 2][:],
                in_=x_t[k][:].rearrange("p (n t) -> p t n", t=PACK)[:, ADDT],
                func=ACT.Copy,
                scale=-1.0,
            )

        def subtract(k, t):
            if on_tensor(k, t):
                nc.scalar.activation(
                    out=slots(diff[k % 2])[:, t], in_=held[("r", k, t)][:], func=ACT.Copy, scale=dec[:, k % FG, t : t + 1]
                )
                return
            nc.vector.scalar_tensor_tensor(
                out=slots(diff[k % 2])[:, t],
                in0=held[("r", k, t)][:],
                scalar=dec[:, k % FG, t : t + 1],
                in1=x_t[k][:].rearrange("p (n t) -> p t n", t=PACK)[:, t],
                op0=ALU.mult,
                op1=ALU.subtract,
            )

        def turn_d(k, s):
            bank = take("bank", banks, ("d", k, s))
            for t in range(PACK):
                terms = [slots(diff[k % 2])[:, t]] + ([minus_x[k % 2][:]] if on_tensor(k, t) else [])
                for n, term in enumerate(terms):
                    nc.tensor.matmul(
                        bank[:, t * P : (t + 1) * P],
                        lhsT=term[:, s * P : (s + 1) * P],
                        rhs=ident[:],
                        start=(n == 0),
                        stop=(n == len(terms) - 1),
                        is_transpose=True,
                    )

        def y_part(k, part, parts):
            width = PACK * GROUP // parts
            return y_f32[k % FG][:, part * width : (part + 1) * width]

        def weigh(k, s, part=0, parts=1):
            ms = slice(part * P // parts, (part + 1) * P // parts)
            nc.vector.tensor_tensor(
                out=y_part(k, part, parts).rearrange("p (s m t) -> p s m t", s=PACK, t=PACK)[:, s],
                in0=held[("d", k, s)][:].rearrange("p (t m) -> p m t", t=PACK)[:, ms],
                in1=slots(rows[k])[:, s].rearrange("p (m t) -> p m t", t=PACK)[:, ms],
                op=ALU.mult,
            )

        def store_y(k, part=0, parts=1):
            tg, fg = divmod(k, FG)
            cols = slice(part * GROUP // parts, (part + 1) * GROUP // parts)
            nc.sync.dma_start(
                out=block(out_0, tg, fg)[:, :, cols], in_=y_part(k, part, parts).rearrange("p (s n) -> p s n", s=PACK)
            )

        def store_rows(k, two):
            tg, fg = divmod(k, FG)
            rows_s = slice(two[0], two[-1] + 1)
            nc.sync.dma_start(out=block(out_0, tg, fg)[:, rows_s], in_=slots(y_f32[k % FG])[:, rows_s])

        def round_y(k, engine, part=0, parts=1):
            dst = take("stage", stage, ("y", k)) if part == 0 else held[("y", k)]
            width = PACK * GROUP // parts
            copy(
                engine,
                dst[:, part * width : (part + 1) * width].rearrange("p (c i s) -> p c s i", i=4, s=PACK),
                y_part(k, part, parts).rearrange("p (s c i) -> p c s i", s=PACK, i=4),
            )

        def quantize_y(k, c0=0, c1=GROUP):
            tg, fg = divmod(k, FG)
            cols = slice(fg * GROUP + c0, fg * GROUP + c1)
            quantize(y_codes[k % 2][:, c0:c1], y_scales[tg][:, cols], held[("y", k)][:, PACK * c0 : PACK * c1])
            nc.sync.dma_start(
                out=out_1[tg, :, cols, :].rearrange("p m t -> p (m t)").bitcast(I32),
                in_=y_codes[k % 2][:, c0:c1].bitcast(I32),
            )

        def store_scales(tg, c0, c1, queues):
            for q in range(4):
                queues[q % len(queues)].dma_start(
                    out=out_2[tg, 4 * q : 4 * q + 4, c0:c1].bitcast(I32),
                    in_=y_scales[tg][32 * q : 32 * q + 4, c0:c1].bitcast(I32),
                )

        def load_gain(dst, src):
            nc.sync.dma_start(out=dst[:], in_=src.rearrange("o (g p t) -> p (o g) t", p=P, t=PACK))


        nc.scalar.dma_start(out=w_scale[:], in_=W_scale.rearrange("(g p t) j -> p g (t j)", p=P, t=PACK))
        make_identity(nc, ident[:])
        nc.vector.memset(warm[:, 0:1], 0.0)
        nc.scalar.activation(out=warm[:, 1:2], in_=warm[:, 0:1], func=ACT.Sigmoid)
        for kind, a, b in FIRST:
            if kind == "w":
                load_w(a, b)
            else:
                load_rows(X, a, b)
        steps = [(fg, hg) for hg in range(HG) for fg in range(FG)]
        widen(0, 0)
        load_w(0, 1)
        for blk in MID:
            load_rows(X, *blk)
        load_gain(enc_raw, enc_gain)
        load_gain(cod_raw, code_gain)
        load_gain(dec_raw, dec_gain)

        def x_blocks(i):
            return [(tg, i - tg * XLAG) for tg in range(TG) if 0 <= i - tg * XLAG < FG]

        for i, (fg, hg) in enumerate(steps):
            if i == 0:
                weave_w(0, 0, 0, "scalar")
                weave_w(0, 0, 1, "vector")
                if WFIRST:
                    turn_w(0, 0)
                    empty_w(0, 0, 0, "scalar")
                    empty_w(0, 0, 1, "scalar")
            if i + 1 < len(steps):
                widen(*steps[i + 1])
                if i + 1 < FG:
                    load_w(i + 1, 1)
                if i == 0:
                    for blk in LATE:
                        load_rows(X, *blk)
            for n, blk in enumerate(x_blocks(i)):
                turn_x(*blk, WX.get(blk, 0))
                if n == 0 and 2 <= i <= FG and SPLIT:
                    for s in range(2, PACK):
                        encode(0, 0, s, i - 2, 0)
            if i == SQ0:
                nc.scalar.copy(out=enc[:], in_=enc_raw[:])
                nc.scalar.copy(out=cod[:], in_=cod_raw[:])
                nc.scalar.copy(out=dec[:], in_=dec_raw[:])
                for s in range(PACK):
                    squash(0, 0, s)
            if i > 0:
                weave_w(fg, hg, 0, "vector" if i in VW0 else "scalar")
                weave_w(fg, hg, 1, "vector" if i in VW else "scalar")
            for blk in x_blocks(i):
                empty_x(*blk, 0, "scalar")
                empty_x(*blk, 1, "scalar")
            if WFIRST <= i < EW:
                turn_w(i, 0, WW[i])
                empty_w(i, 0, 0, "scalar")
                empty_w(i, 0, 1, "scalar")
            if i == 0:
                quantize_enc(0, 0)
            if i > 1:
                quantize_enc(*steps[i - 1])
            if i > 0:
                for blk in x_blocks(i - 1):
                    quantize_x(*blk)
                if i <= QD:
                    quantize_dec(i - 1, 0)
                if i <= FG:
                    for s in range(2 if i < FG and SPLIT else PACK):
                        encode(0, 0, s, i - 1, 0)
            if i == FG:
                for g in range(FG - XLAG):
                    for s in range(PACK):
                        encode(1, 0, s, g, PACK)
            if i == FG + 1 and XLAG:
                for s in range(PACK):
                    encode(1, 0, s, FG - 1, PACK)
            if i > FG:
                for s in range(PACK):
                    encode(0, 1, s, i - 1 - FG, 0)
            if i == SQ1:
                for s in range(PACK):
                    squash(1, 0, s)
        for k in range(TG * FG):
            load_rows(V, *divmod(k, FG))
        quantize_enc(FG - 1, 1)
        for s in range(PACK):
            encode(0, 1, s, FG - 1, 0)
        make_code(0, 0, 0)
        make_code(0, 0, 1)
        for fg in range(QD, FG):
            quantize_dec(fg, 0)
        for half in range(2):
            for s in range(PACK):
                squash(0, 1, s, slice(half * 256, half * 256 + 256))
        for fg in range(2):
            turn_w(fg, 1)
            empty_w(fg, 1, 0, "scalar")
            empty_w(fg, 1, 1, "scalar")
        for s in range(PACK):
            for fg in range(FG):
                encode(1, 1, s, fg)
        make_code(0, 1, 0)
        quantize_c(0, 0)
        make_code(0, 1, 1)
        for s in range(PACK):
            squash(1, 1, s)
        quantize_dec(0, 1)
        quantize_c(0, 1)
        quantize_dec(1, 1)
        units = TG * FG
        for k in range(-1, units - 1):
            last = k + 1 == units
            for pair in range(2):
                two = range(2 * pair, 2 * pair + 2)
                if not last:
                    for t in two:
                        decode(k + 1, t)
                        subtract(k + 1, t)
                if pair == 0 and 0 <= k < FG - 2:
                    for hg in range(0 if k + 2 >= EW else 1, HG):
                        turn_w(k + 2, hg)
                        empty_w(k + 2, hg, 0, "scalar")
                        empty_w(k + 2, hg, 1, "scalar")
                if pair == 1:
                    if k in (1, 2):
                        quantize_c(1, k - 1)
                    if 0 <= k < FG - 2:
                        for hg in range(0 if k + 2 >= EW else 1, HG):
                            quantize_dec(k + 2, hg)
                    for j in QY.get(k, []):
                        quantize_y(j)
                        if j == FG - 1:
                            store_scales(0, 0, F, [nc.sync])
                if k >= 0:
                    for s in two:
                        turn_d(k, s)
                        if not last:
                            weigh(k, s)
                    store_rows(k, two)
            if k in (-1, 0):
                for s in range(PACK):
                    scale_code(1, k + 1, s)
                weave_code(1, k + 1, "scalar")
            if ADD0 <= k + 2 < ADD1:
                negate_x(k + 2)
            for j in RY.get(k, []):
                round_y(j, "scalar")
        k = units - 1
        store_scales(1, 0, F // 2, [nc.sync])
        for s in range(PACK):
            turn_d(k, s)
        for half in range(2):
            for s in range(PACK):
                weigh(k, s, half, 2)
            store_y(k, half, 2)
        round_y(k, "scalar", 0, 2)
        quantize_y(k - 1)
        round_y(k, "vector", 1, 2)
        quantize_y(k, 0, 256)
        quantize_y(k, 256, 512)
        store_scales(1, F // 2, F, [nc.scalar, nc.sync])
